import numpy as np
import ml_dtypes


def mxq(x, axis, fmt="e4m3"):
    dtype, down = {"e4m3": (ml_dtypes.float8_e4m3fn, 7), "e5m2": (ml_dtypes.float8_e5m2, 14)}[fmt]
    v = np.moveaxis(np.asarray(x, np.float32).astype(ml_dtypes.bfloat16).astype(np.float64), axis, -1)
    blocks = v.reshape(v.shape[:-1] + (-1, 32))
    amax = np.abs(blocks).max(-1, keepdims=True)
    byte = np.maximum(np.where(amax > 0, np.frexp(amax)[1] - 1 + 127, 0) - down, 1)
    scale = np.exp2(byte - 127.0)
    codes = (blocks / scale).astype(np.float32).astype(dtype).astype(np.float64)
    return np.moveaxis((codes * scale).reshape(v.shape), -1, axis)


WIDE = False


def mx_kscale(k):
    if not WIDE:
        return np.ones(k)
    levels = np.array([30, -30])
    if k % 512:
        return np.exp2(np.random.permutation(np.resize(levels, k // 32))).repeat(32)
    a = np.empty((k // 512, 16))
    for p in range(k // 512):
        a[p, :8] = np.random.permutation(np.resize(levels, 8))
        for g in range(8):
            far = levels[np.abs(levels - a[p, g]) >= 10]
            a[p, g + 8] = far[np.random.randint(len(far))]
    return np.exp2(a.ravel()).repeat(32)


def f64(x):
    return np.asarray(x).astype(np.float64)


def striped(idx):
    return np.tile(np.asarray(idx).reshape(-1, 16).T, (8, 1)).astype(np.uint16)


def unstriped(offs):
    return offs[:16].T.reshape(-1).astype(np.int64)


def striped8(idx):
    return np.asarray(idx).reshape(8, -1, 16).transpose(0, 2, 1).reshape(128, -1).astype(np.uint16)


def unstriped8(offs):
    return offs.reshape(8, 16, -1).transpose(0, 2, 1).reshape(8, -1).astype(np.int64)


def pick8(x, idx, run):
    r = np.arange(len(x))
    return x[r[:, None], idx[r % (8 * run) // run]]


E2M1 = np.array([0.0, 0.5, 1.0, 1.5, 2.0, 3.0, 4.0, 6.0, -0.0, -0.5, -1.0, -1.5, -2.0, -3.0, -4.0, -6.0])


def pack_weight(w, fmt):
    k, n = w.shape
    w = f64(np.asarray(w, np.float32).astype(ml_dtypes.bfloat16)).reshape(k // 32, 32, n)
    amax = np.abs(w).max(1)
    if fmt in ("e4m3", "e5m2"):
        byte = np.frexp(amax)[1] - 1 + 127 - (7 if fmt == "e4m3" else 14)
    else:
        mant, ex = np.frexp(amax / 6.0)
        byte = np.where(mant > 0.5, ex, ex - 1) + 127
    byte = np.clip(np.where(amax > 0, byte, 1), 1, 254)
    scaled = (w * np.exp2(127.0 - byte)[:, None, :]).reshape(k, n).astype(np.float32)
    by_word = np.ascontiguousarray(scaled.reshape(k // 512, 128, 4, n).transpose(0, 1, 3, 2))
    if fmt in ("e4m3", "e5m2"):
        words = by_word.astype(ml_dtypes.float8_e4m3fn if fmt == "e4m3" else ml_dtypes.float8_e5m2).view(np.uint8)
    else:
        c = by_word.astype(ml_dtypes.float4_e2m1fn).view(np.uint8) & 0xF
        words = (c[..., 0::2] | (c[..., 1::2] << 4)).reshape(k // 512, 128, 2 * n)
    return np.ascontiguousarray(words), np.ascontiguousarray(byte.astype(np.uint8).reshape(k // 512, 16, n))


def unpack_weight(words, scales, fmt):
    g, _, n = scales.shape
    words = np.ascontiguousarray(words).reshape(g, 128, n, -1)
    if fmt in ("e4m3", "e5m2"):
        vals = words.view(ml_dtypes.float8_e4m3fn if fmt == "e4m3" else ml_dtypes.float8_e5m2).astype(np.float64)
    else:
        nib = np.empty((g, 128, n, 4), np.uint8)
        nib[..., 0::2] = words & 0xF
        nib[..., 1::2] = words >> 4
        vals = E2M1[nib]
    vals = vals * np.repeat(np.exp2(scales.astype(np.float64) - 127.0), 8, axis=1)[..., None]
    return vals.transpose(0, 1, 3, 2).reshape(g * 512, n)


K, T, J, R, C, O, U, D, N, E = 512, 1024, 256, 512, 512, 128, 128, 256, 256, 1024


def setup_inputs():
    n = np.random.standard_normal
    idx = np.random.permutation(T)[:J]
    idx2 = np.stack([np.random.permutation(C)[:J] for _ in range(8)])
    idx3 = np.random.permutation(C)[:O]
    idx4 = np.random.permutation(C)[:U]
    idx5 = np.random.permutation(T)[:D]
    idx6 = np.random.permutation(E)[:D]
    fk = mx_kscale(K)
    fr = mx_kscale(R)
    xtp = pack_weight(n((K, T)) / fk[:, None], "e5m2")
    wp = pack_weight(n((K, R)) * 1 / np.sqrt(K) * fk[:, None] * fr, "e2m1")
    wbp = pack_weight(n((R, N)) * 1 / np.sqrt(R) / fr[:, None], "e2m1")
    wsp = pack_weight(n((K, N)) * 1 / np.sqrt(K) * fk[:, None], "e2m1")
    return {
        "xt_words": xtp[0],
        "xt_scales": xtp[1],
        "w_words": wp[0],
        "w_scales": wp[1],
        "sa": (np.random.uniform(0.5, 1.6, (R, 1))).astype(np.float32),
        "sb": (np.random.uniform(0.5, 1.6, (R, 1))).astype(np.float32),
        "wb_words": wbp[0],
        "wb_scales": wbp[1],
        "ws_words": wsp[0],
        "ws_scales": wsp[1],
        "offs": striped(idx),
        "offs2": striped8(idx2),
        "offs3": striped(idx3),
        "offs4": striped(idx4),
        "offs5": striped(idx5),
        "offs6": striped(idx6),
    }


def reference(xt_words, xt_scales, w_words, w_scales, sa, sb, wb_words, wb_scales, ws_words, ws_scales, offs, offs2, offs3, offs4, offs5, offs6):
    idx = unstriped(offs)
    idx2 = unstriped8(offs2)
    idx3 = unstriped(offs3)
    idx4 = unstriped(offs4)
    idx5 = unstriped(offs5)
    idx6 = unstriped(offs6)
    xtu = unpack_weight(xt_words, xt_scales, "e5m2")
    wu = unpack_weight(w_words, w_scales, "e2m1")
    wbu = unpack_weight(wb_words, wb_scales, "e2m1")
    wsu = unpack_weight(ws_words, ws_scales, "e2m1")
    xtidxg = xtu[:, idx]
    a = wu.T @ xtidxg
    pw = np.zeros((R, C))
    pw[np.arange(R)[:, None], idx2[np.arange(R) % 512 // 64]] = a
    h1 = pw[:, idx3] * f64(sa)
    h2 = pw[:, idx4] * f64(sb)
    hid = np.concatenate([h1, h2], axis=1)
    hidq = mxq(hid, 0, "e4m3")
    xtidx5g = xtu[:, idx5]
    p = wbu.T @ hidq + wsu.T @ xtidx5g
    y = np.zeros((N, E))
    y[:, idx6] = p
    return y

@@ -1,0 +1,183 @@
+from contextlib import ExitStack
+
+import concourse.mybir as mybir
+
+K, T, J, R, C, O, U, D, N, E = 512, 1024, 256, 512, 512, 128, 128, 256, 256, 1024
+FLOPS = 2 * K * R * J + 2 * R * N * D + 2 * K * N * D
+
+F32 = mybir.dt.float32
+BF16 = mybir.dt.bfloat16
+I32 = mybir.dt.int32
+U32 = mybir.dt.uint32
+U16 = mybir.dt.uint16
+U8 = mybir.dt.uint8
+E4M3 = mybir.dt.float8_e4m3fn_x4
+E5M2 = mybir.dt.float8_e5m2_x4
+E2M1 = mybir.dt.float4_e2m1fn_x4
+COPY = mybir.ActivationFunctionType.Copy
+
+P = 128
+PACK = 4
+QUADS = 4
+HALF = 128
+
+
+def load_scale_rows(queues, plane, scales):
+    for q in range(QUADS):
+        queues[q].dma_start(out=plane[32 * q : 32 * q + 4, :].bitcast(I32), in_=scales[0, 4 * q : 4 * q + 4, :].bitcast(I32))
+
+
+def tile_list_ownsides_solo_further_scattered_kernel(
+    tc, xt_words, xt_scales, w_words, w_scales, sa, sb, wb_words, wb_scales, ws_words, ws_scales,
+    offs, offs2, offs3, offs4, offs5, offs6, out,
+):
+    nc = tc.nc
+    with ExitStack() as ctx:
+        keep = ctx.enter_context(tc.tile_pool(name="keep", bufs=1))
+        psum = ctx.enter_context(tc.psum_pool(name="psum", bufs=1))
+
+        slots = keep.tile([P, J // 16], U16, name="slots")
+        board_cols = keep.tile([P, J // 16], U16, name="board_cols")
+        places = keep.tile([P, O // 16], U16, name="places")
+        late_places = keep.tile([P, U // 16], U16, name="late_places")
+        short_tokens = keep.tile([P, D // 16], U16, name="short_tokens")
+        page_cols = keep.tile([P, D // 16], U16, name="page_cols")
+
+        x_words = keep.tile([P, T], I32, name="x_words", tag="x_words_then_page", align_bytes=64)
+        x_plane = keep.tile([P, T], U8, name="x_plane", tag="x_plane_then_page", align_bytes=64)
+        w_raw = keep.tile([P, 2 * R], U8, name="w_raw", align_bytes=64)
+        w_rows = keep.tile([4, QUADS, R // 4], I32, name="w_rows", align_bytes=64)
+        w_plane_raw = keep.tile([P, R], U8, name="w_plane_raw", align_bytes=64)
+        wb_codes = keep.tile([P, 2 * N], U8, name="wb_codes", align_bytes=64)
+        wb_plane = keep.tile([P, N], U8, name="wb_plane", align_bytes=64)
+        ws_codes = keep.tile([P, 2 * N], U8, name="ws_codes", align_bytes=64)
+        ws_plane = keep.tile([P, N], U8, name="ws_plane", align_bytes=64)
+        sa_cols = keep.tile([P, PACK], F32, name="sa_cols")
+        sb_cols = keep.tile([P, PACK], F32, name="sb_cols")
+
+        nc.vector.memset(x_plane[:].bitcast(I32), 0)
+        nc.vector.memset(w_plane_raw[:].bitcast(I32), 0)
+
+        x_words_hbm = xt_words[0].rearrange("p n t -> p (n t)").bitcast(I32)
+        nc.sync.dma_start(slots[:], offs)
+        nc.scalar.dma_start(out=x_words[:, 0 : T // 2], in_=x_words_hbm[:, 0 : T // 2])
+        nc.sync.dma_start(out=w_rows[:], in_=w_scales[0].bitcast(I32).rearrange("(q r) c -> r q c", r=4))
+        load_scale_rows([nc.sync, nc.scalar, nc.sync, nc.scalar], x_plane, xt_scales)
+        nc.sync.dma_start(out=x_words[:, T // 2 : T], in_=x_words_hbm[:, T // 2 : T])
+        nc.sync.dma_start(out=w_raw[:].bitcast(I32), in_=w_words[0].bitcast(I32))
+        nc.sync.dma_start(board_cols[:], offs2)
+        nc.sync.dma_start(places[:], offs3)
+        nc.sync.dma_start(out=sa_cols[:], in_=sa.rearrange("(p t) o -> p (t o)", t=PACK))
+        nc.sync.dma_start(short_tokens[:], offs5)
+        nc.sync.dma_start(out=ws_codes[:].bitcast(I32), in_=ws_words[0].bitcast(I32))
+        nc.sync.dma_start(late_places[:], offs4)
+        nc.sync.dma_start(out=sb_cols[:], in_=sb.rearrange("(p t) o -> p (t o)", t=PACK))
+        nc.sync.dma_start(out=wb_codes[:].bitcast(I32), in_=wb_words[0].bitcast(I32))
+
+        boards = []
+        for t in range(PACK):
+            board = keep.tile([P, C], F32, name="board%d" % t)
+            nc.vector.memset(board[:], 0.0)
+            boards.append(board)
+        nc.vector.memset(ws_plane[:].bitcast(I32), 0)
+        nc.vector.memset(wb_plane[:].bitcast(I32), 0)
+        load_scale_rows([nc.sync] * QUADS, ws_plane, ws_scales)
+        load_scale_rows([nc.sync] * QUADS, wb_plane, wb_scales)
+        nc.sync.dma_start(page_cols[:], offs6)
+
+        for q in range(QUADS):
+            nc.vector.tensor_copy(out=w_plane_raw[32 * q : 32 * q + 4, :].bitcast(I32), in_=w_rows[:, q, :])
+
+        xg_plane = keep.tile([P, J], U8, name="xg_plane", align_bytes=64)
+        xg_words = keep.tile([P, J], U32, name="xg_words", align_bytes=64)
+        nc.vector.tensor_copy(out=xg_plane[:], in_=x_plane[:].indirect(slots[:]))
+
+        w_codes = []
+        w_planes = []
+
+        def deal(t):
+            codes = keep.tile([P, 2 * P], U8, name="w_codes%d" % t, align_bytes=64)
+            plane = keep.tile([P, P], U8, name="w_plane%d" % t, align_bytes=64)
+            nc.vector.tensor_copy(out=plane[:], in_=w_plane_raw[:, t::PACK])
+            nc.scalar.copy(out=codes[:].bitcast(U16), in_=w_raw[:].bitcast(U16)[:, t::PACK])
+            w_codes.append(codes)
+            w_planes.append(plane)
+
+        deal(0)
+        nc.vector.tensor_copy(out=xg_words[:], in_=x_words[:].bitcast(U32).indirect(slots[:]))
+
+        hid = [keep.tile([P, PACK, HALF], BF16, name="hid0", align_bytes=64)]
+        for t in range(PACK):
+            if t > 0:
+                deal(t)
+            acc = psum.tile([P, J], F32, name="a_acc%d" % t)
+            nc.tensor.matmul_mx(
+                out=acc[:], lhsT=w_codes[t][:].bitcast(E2M1), lhsT_scale=w_planes[t][:],
+                rhs=xg_words[:].bitcast(E5M2), rhs_scale=xg_plane[:], start=True, stop=True,
+            )
+            a_rows = keep.tile([P, J], F32, name="a_rows%d" % t, tag="a_rows%d" % t, align_bytes=64)
+            nc.vector.tensor_copy(out=a_rows[:], in_=acc[:])
+            nc.scalar.activation(out=boards[t][:].indirect(board_cols[:]), in_=a_rows[:], func=COPY)
+            nc.scalar.activation(
+                out=hid[0][:, t, :], in_=boards[t][:].indirect(places[:]), func=COPY, scale=sa_cols[:, t : t + 1]
+            )
+
+        xs_plane = keep.tile([P, D], U8, name="xs_plane", align_bytes=64)
+        xs_words = keep.tile([P, D], U32, name="xs_words", align_bytes=64)
+        nc.vector.tensor_copy(out=xs_plane[:], in_=x_plane[:].indirect(short_tokens[:]))
+        nc.vector.tensor_copy(out=xs_words[:], in_=x_words[:].bitcast(U32).indirect(short_tokens[:]))
+        p_acc = {}
+        for h in range(2):
+            cols = slice(h * HALF, (h + 1) * HALF)
+            for i in range(2):
+                acc = psum.tile([P, HALF], F32, name="p_acc%d%d" % (h, i))
+                nc.tensor.matmul_mx(
+                    out=acc[:], lhsT=ws_codes[:, 2 * P * i : 2 * P * (i + 1)].bitcast(E2M1),
+                    lhsT_scale=ws_plane[:, P * i : P * (i + 1)],
+                    rhs=xs_words[:, cols].bitcast(E5M2), rhs_scale=xs_plane[:, cols], start=True, stop=False,
+                )
+                p_acc[(h, i)] = acc
+
+        page0 = keep.tile([P, E], F32, name="page0", tag="x_words_then_page", align_bytes=64)
+        page1 = keep.tile([P, E], F32, name="page1", tag="x_plane_then_page", align_bytes=64)
+        pages = [page0, page1]
+        for page in pages:
+            nc.vector.memset(page[:], 0.0)
+
+        hid.append(keep.tile([P, PACK, HALF], BF16, name="hid1", tag="a_rows%d" % (PACK - 1), align_bytes=64))
+        for t in range(PACK):
+            nc.scalar.activation(
+                out=hid[1][:, t, :], in_=boards[t][:].indirect(late_places[:]), func=COPY, scale=sb_cols[:, t : t + 1]
+            )
+
+        def second_stage(h):
+            grouped = keep.tile([P, HALF, PACK], BF16, name="grouped%d" % h, tag="grouped", align_bytes=64)
+            nc.vector.tensor_copy(
+                out=grouped[:].rearrange("p (c i) t -> p c t i", i=4),
+                in_=hid[h][:].rearrange("p t (c i) -> p c t i", i=4),
+            )
+            codes = keep.tile([P, HALF], U32, name="hid_codes%d" % h, align_bytes=64)
+            plane = keep.tile([P, HALF], U8, name="hid_plane%d" % h, align_bytes=64)
+            nc.vector.quantize_mx(out=codes[:].bitcast(E4M3), scales=plane[:], in_=grouped[:].rearrange("p d t -> p (d t)"))
+            for i in (1, 0):
+                nc.tensor.matmul_mx(
+                    out=p_acc[(h, i)][:], lhsT=wb_codes[:, 2 * P * i : 2 * P * (i + 1)].bitcast(E2M1),
+                    lhsT_scale=wb_plane[:, P * i : P * (i + 1)],
+                    rhs=codes[:].bitcast(E4M3), rhs_scale=plane[:], start=False, stop=True,
+                )
+
+        def put(h):
+            entries = page_cols[:, h * (HALF // 16) : (h + 1) * (HALF // 16)]
+            rows1 = keep.tile([P, HALF], F32, name="p_rows%d1" % h)
+            nc.scalar.copy(out=rows1[:], in_=p_acc[(h, 1)][:])
+            rows0 = keep.tile([P, HALF], F32, name="p_rows%d0" % h)
+            nc.scalar.copy(out=rows0[:], in_=p_acc[(h, 0)][:])
+            nc.scalar.activation(out=page0[:].indirect(entries), in_=rows0[:], func=COPY)
+            nc.vector.tensor_copy(out=page1[:].indirect(entries), in_=rows1[:])
+
+        second_stage(0)
+        second_stage(1)
+        put(0)
+        put(1)
+        nc.sync.dma_start(out=out[0:P, :], in_=page0[:])
+        nc.sync.dma_start(out=out[P : 2 * P, :], in_=page1[:])

@@ -46,7 +46,7 @@ def tile_list_ownsides_solo_further_scattered_kernel(
         x_words = keep.tile([P, T], I32, name="x_words", tag="x_words_then_page", align_bytes=64)
         x_plane = keep.tile([P, T], U8, name="x_plane", tag="x_plane_then_page", align_bytes=64)
         w_raw = keep.tile([P, 2 * R], U8, name="w_raw", align_bytes=64)
-        w_rows = keep.tile([4, QUADS, R // 4], I32, name="w_rows", align_bytes=64)
+        w_rows = keep.tile([4, QUADS, R // 4], I32, name="w_rows", tag="w_rows_then_words", align_bytes=64)
         w_plane_raw = keep.tile([P, R], U8, name="w_plane_raw", align_bytes=64)
         wb_codes = keep.tile([P, 2 * N], U8, name="wb_codes", align_bytes=64)
         wb_plane = keep.tile([P, N], U8, name="wb_plane", align_bytes=64)
@@ -60,11 +60,10 @@ def tile_list_ownsides_solo_further_scattered_kernel(
 
         x_words_hbm = xt_words[0].rearrange("p n t -> p (n t)").bitcast(I32)
         nc.sync.dma_start(slots[:], offs)
-        nc.scalar.dma_start(out=x_words[:, 0 : T // 2], in_=x_words_hbm[:, 0 : T // 2])
+        nc.scalar.dma_start(out=w_raw[:].bitcast(I32), in_=w_words[0].bitcast(I32))
         nc.sync.dma_start(out=w_rows[:], in_=w_scales[0].bitcast(I32).rearrange("(q r) c -> r q c", r=4))
-        load_scale_rows([nc.sync, nc.scalar, nc.sync, nc.scalar], x_plane, xt_scales)
-        nc.sync.dma_start(out=x_words[:, T // 2 : T], in_=x_words_hbm[:, T // 2 : T])
-        nc.sync.dma_start(out=w_raw[:].bitcast(I32), in_=w_words[0].bitcast(I32))
+        nc.scalar.dma_start(out=x_words[:], in_=x_words_hbm)
+        load_scale_rows([nc.sync] * QUADS, x_plane, xt_scales)
         nc.sync.dma_start(board_cols[:], offs2)
         nc.sync.dma_start(places[:], offs3)
         nc.sync.dma_start(out=sa_cols[:], in_=sa.rearrange("(p t) o -> p (t o)", t=PACK))
@@ -73,6 +72,7 @@ def tile_list_ownsides_solo_further_scattered_kernel(
         nc.sync.dma_start(late_places[:], offs4)
         nc.sync.dma_start(out=sb_cols[:], in_=sb.rearrange("(p t) o -> p (t o)", t=PACK))
         nc.sync.dma_start(out=wb_codes[:].bitcast(I32), in_=wb_words[0].bitcast(I32))
+        nc.sync.dma_start(page_cols[:], offs6)
 
         boards = []
         for t in range(PACK):
@@ -83,14 +83,12 @@ def tile_list_ownsides_solo_further_scattered_kernel(
         nc.vector.memset(wb_plane[:].bitcast(I32), 0)
         load_scale_rows([nc.sync] * QUADS, ws_plane, ws_scales)
         load_scale_rows([nc.sync] * QUADS, wb_plane, wb_scales)
-        nc.sync.dma_start(page_cols[:], offs6)
 
         for q in range(QUADS):
             nc.vector.tensor_copy(out=w_plane_raw[32 * q : 32 * q + 4, :].bitcast(I32), in_=w_rows[:, q, :])
 
         xg_plane = keep.tile([P, J], U8, name="xg_plane", align_bytes=64)
-        xg_words = keep.tile([P, J], U32, name="xg_words", align_bytes=64)
-        nc.vector.tensor_copy(out=xg_plane[:], in_=x_plane[:].indirect(slots[:]))
+        xg_words = keep.tile([P, J], U32, name="xg_words", tag="w_rows_then_words", align_bytes=64)
 
         w_codes = []
         w_planes = []
@@ -103,21 +101,33 @@ def tile_list_ownsides_solo_further_scattered_kernel(
             w_codes.append(codes)
             w_planes.append(plane)
 
-        deal(0)
-        nc.vector.tensor_copy(out=xg_words[:], in_=x_words[:].bitcast(U32).indirect(slots[:]))
-
-        hid = [keep.tile([P, PACK, HALF], BF16, name="hid0", align_bytes=64)]
-        for t in range(PACK):
-            if t > 0:
-                deal(t)
-            acc = psum.tile([P, J], F32, name="a_acc%d" % t)
+        def first_product(t, first, count, tag, copy_out):
+            cols = slice(first, first + count)
+            acc = psum.tile([P, count], F32, name="a_acc%d_%d" % (t, first), tag=tag)
             nc.tensor.matmul_mx(
                 out=acc[:], lhsT=w_codes[t][:].bitcast(E2M1), lhsT_scale=w_planes[t][:],
-                rhs=xg_words[:].bitcast(E5M2), rhs_scale=xg_plane[:], start=True, stop=True,
+                rhs=xg_words[:, cols].bitcast(E5M2), rhs_scale=xg_plane[:, cols], start=True, stop=True,
             )
-            a_rows = keep.tile([P, J], F32, name="a_rows%d" % t, tag="a_rows%d" % t, align_bytes=64)
-            nc.vector.tensor_copy(out=a_rows[:], in_=acc[:])
-            nc.scalar.activation(out=boards[t][:].indirect(board_cols[:]), in_=a_rows[:], func=COPY)
+            a_rows = keep.tile([P, count], F32, name="a_rows%d_%d" % (t, first), tag="a_rows%d_%d" % (t, first), align_bytes=64)
+            copy_out(out=a_rows[:], in_=acc[:])
+            entries = board_cols[:, first // 16 : (first + count) // 16]
+            nc.scalar.activation(out=boards[t][:].indirect(entries), in_=a_rows[:], func=COPY)
+
+        deal(0)
+        for first in (0, HALF):
+            entries = slots[:, first // 16 : (first + HALF) // 16]
+            nc.vector.tensor_copy(out=xg_plane[:, first : first + HALF], in_=x_plane[:].indirect(entries))
+            nc.vector.tensor_copy(out=xg_words[:, first : first + HALF], in_=x_words[:].bitcast(U32).indirect(entries))
+            first_product(0, first, HALF, "bank_a0_%d" % first, nc.scalar.copy if first == 0 else nc.vector.tensor_copy)
+            if first == 0:
+                deal(1)
+            first_product(1, first, HALF, "bank_a1_%d" % first, nc.vector.tensor_copy)
+        for t in range(2, PACK):
+            deal(t)
+            first_product(t, 0, J, "bank_a%d" % t, nc.vector.tensor_copy)
+
+        hid = [keep.tile([P, PACK, HALF], BF16, name="hid0", tag="a_rows2_0", align_bytes=64)]
+        for t in range(PACK):
             nc.scalar.activation(
                 out=hid[0][:, t, :], in_=boards[t][:].indirect(places[:]), func=COPY, scale=sa_cols[:, t : t + 1]
             )
@@ -130,7 +140,7 @@ def tile_list_ownsides_solo_further_scattered_kernel(
         for h in range(2):
             cols = slice(h * HALF, (h + 1) * HALF)
             for i in range(2):
-                acc = psum.tile([P, HALF], F32, name="p_acc%d%d" % (h, i))
+                acc = psum.tile([P, HALF], F32, name="p_acc%d%d" % (h, i), tag="bank_a%d_0" % i if h == 1 else "bank_p%d" % i)
                 nc.tensor.matmul_mx(
                     out=acc[:], lhsT=ws_codes[:, 2 * P * i : 2 * P * (i + 1)].bitcast(E2M1),
                     lhsT_scale=ws_plane[:, P * i : P * (i + 1)],
@@ -144,40 +154,48 @@ def tile_list_ownsides_solo_further_scattered_kernel(
         for page in pages:
             nc.vector.memset(page[:], 0.0)
 
-        hid.append(keep.tile([P, PACK, HALF], BF16, name="hid1", tag="a_rows%d" % (PACK - 1), align_bytes=64))
+        hid.append(keep.tile([P, PACK, HALF], BF16, name="hid1", tag="a_rows%d_0" % (PACK - 1), align_bytes=64))
         for t in range(PACK):
             nc.scalar.activation(
                 out=hid[1][:, t, :], in_=boards[t][:].indirect(late_places[:]), func=COPY, scale=sb_cols[:, t : t + 1]
             )
 
         def second_stage(h):
-            grouped = keep.tile([P, HALF, PACK], BF16, name="grouped%d" % h, tag="grouped", align_bytes=64)
-            nc.vector.tensor_copy(
-                out=grouped[:].rearrange("p (c i) t -> p c t i", i=4),
-                in_=hid[h][:].rearrange("p t (c i) -> p c t i", i=4),
-            )
             codes = keep.tile([P, HALF], U32, name="hid_codes%d" % h, align_bytes=64)
             plane = keep.tile([P, HALF], U8, name="hid_plane%d" % h, align_bytes=64)
-            nc.vector.quantize_mx(out=codes[:].bitcast(E4M3), scales=plane[:], in_=grouped[:].rearrange("p d t -> p (d t)"))
-            for i in (1, 0):
+            parts = []
+            for s in range(2):
+                grouped = keep.tile([P, HALF // 2, PACK], BF16, name="grouped%d%d" % (h, s), tag="grouped%d" % s, align_bytes=64)
+                cols = slice(s * (HALF // 2), (s + 1) * (HALF // 2))
+                nc.vector.tensor_copy(
+                    out=grouped[:].rearrange("p (c i) t -> p c t i", i=4),
+                    in_=hid[h][:, :, cols].rearrange("p t (c i) -> p c t i", i=4),
+                )
+                parts.append((grouped, cols))
+            for grouped, cols in parts:
+                nc.vector.quantize_mx(
+                    out=codes[:, cols].bitcast(E4M3), scales=plane[:, cols], in_=grouped[:].rearrange("p d t -> p (d t)")
+                )
+            for i in range(2):
                 nc.tensor.matmul_mx(
                     out=p_acc[(h, i)][:], lhsT=wb_codes[:, 2 * P * i : 2 * P * (i + 1)].bitcast(E2M1),
                     lhsT_scale=wb_plane[:, P * i : P * (i + 1)],
                     rhs=codes[:].bitcast(E4M3), rhs_scale=plane[:], start=False, stop=True,
                 )
 
-        def put(h):
+        def put(h, rows0, rows1):
             entries = page_cols[:, h * (HALF // 16) : (h + 1) * (HALF // 16)]
-            rows1 = keep.tile([P, HALF], F32, name="p_rows%d1" % h)
-            nc.scalar.copy(out=rows1[:], in_=p_acc[(h, 1)][:])
-            rows0 = keep.tile([P, HALF], F32, name="p_rows%d0" % h)
-            nc.scalar.copy(out=rows0[:], in_=p_acc[(h, 0)][:])
-            nc.scalar.activation(out=page0[:].indirect(entries), in_=rows0[:], func=COPY)
-            nc.vector.tensor_copy(out=page1[:].indirect(entries), in_=rows1[:])
+            nc.scalar.copy(out=rows0, in_=p_acc[(h, 0)][:])
+            nc.scalar.copy(out=rows1, in_=p_acc[(h, 1)][:])
+            nc.scalar.activation(out=page0[:].indirect(entries), in_=rows0, func=COPY)
+            nc.vector.tensor_copy(out=page1[:].indirect(entries), in_=rows1)
 
         second_stage(0)
         second_stage(1)
-        put(0)
-        put(1)
-        nc.sync.dma_start(out=out[0:P, :], in_=page0[:])
+        early0 = keep.tile([P, HALF], F32, name="early0", tag="p_rows")
+        early1 = keep.tile([P, HALF], F32, name="early1")
+        put(0, early0[:], early1[:])
+        late = keep.tile([P, 2, HALF], F32, name="late", tag="p_rows")
+        put(1, late[:, 0, :], late[:, 1, :])
         nc.sync.dma_start(out=out[P : 2 * P, :], in_=page1[:])
+        nc.scalar.dma_start(out=out[0:P, :], in_=page0[:])

@@ -27,6 +27,11 @@ def load_scale_rows(queues, plane, scales):
         queues[q].dma_start(out=plane[32 * q : 32 * q + 4, :].bitcast(I32), in_=scales[0, 4 * q : 4 * q + 4, :].bitcast(I32))
 
 
+def spread_scale_rows(nc, plane, rows):
+    for q in range(QUADS):
+        nc.vector.tensor_copy(out=plane[32 * q : 32 * q + 4, :].bitcast(I32), in_=rows[:, q, :])
+
+
 def tile_list_ownsides_solo_further_scattered_kernel(
     tc, xt_words, xt_scales, w_words, w_scales, sa, sb, wb_words, wb_scales, ws_words, ws_scales,
     offs, offs2, offs3, offs4, offs5, offs6, out,
@@ -46,12 +51,14 @@ def tile_list_ownsides_solo_further_scattered_kernel(
         x_words = keep.tile([P, T], I32, name="x_words", tag="x_words_then_page", align_bytes=64)
         x_plane = keep.tile([P, T], U8, name="x_plane", tag="x_plane_then_page", align_bytes=64)
         w_raw = keep.tile([P, 2 * R], U8, name="w_raw", align_bytes=64)
-        w_rows = keep.tile([4, QUADS, R // 4], I32, name="w_rows", tag="w_rows_then_words", align_bytes=64)
+        w_rows = keep.tile([4, QUADS, R // 4], I32, name="w_rows", align_bytes=64)
         w_plane_raw = keep.tile([P, R], U8, name="w_plane_raw", align_bytes=64)
         wb_codes = keep.tile([P, 2 * N], U8, name="wb_codes", align_bytes=64)
         wb_plane = keep.tile([P, N], U8, name="wb_plane", align_bytes=64)
         ws_codes = keep.tile([P, 2 * N], U8, name="ws_codes", align_bytes=64)
         ws_plane = keep.tile([P, N], U8, name="ws_plane", align_bytes=64)
+        ws_rows = keep.tile([4, QUADS, N // 4], I32, name="ws_rows", align_bytes=64)
+        wb_rows = keep.tile([4, QUADS, N // 4], I32, name="wb_rows", tag="grouped", align_bytes=64)
         sa_cols = keep.tile([P, PACK], F32, name="sa_cols")
         sb_cols = keep.tile([P, PACK], F32, name="sb_cols")
 
@@ -59,11 +66,11 @@ def tile_list_ownsides_solo_further_scattered_kernel(
         nc.vector.memset(w_plane_raw[:].bitcast(I32), 0)
 
         x_words_hbm = xt_words[0].rearrange("p n t -> p (n t)").bitcast(I32)
-        nc.sync.dma_start(slots[:], offs)
-        nc.scalar.dma_start(out=w_raw[:].bitcast(I32), in_=w_words[0].bitcast(I32))
         nc.sync.dma_start(out=w_rows[:], in_=w_scales[0].bitcast(I32).rearrange("(q r) c -> r q c", r=4))
         nc.scalar.dma_start(out=x_words[:], in_=x_words_hbm)
         load_scale_rows([nc.sync] * QUADS, x_plane, xt_scales)
+        nc.sync.dma_start(slots[:], offs)
+        nc.sync.dma_start(out=w_raw[:].bitcast(I32), in_=w_words[0].bitcast(I32))
         nc.sync.dma_start(board_cols[:], offs2)
         nc.sync.dma_start(places[:], offs3)
         nc.sync.dma_start(out=sa_cols[:], in_=sa.rearrange("(p t) o -> p (t o)", t=PACK))
@@ -72,6 +79,8 @@ def tile_list_ownsides_solo_further_scattered_kernel(
         nc.sync.dma_start(late_places[:], offs4)
         nc.sync.dma_start(out=sb_cols[:], in_=sb.rearrange("(p t) o -> p (t o)", t=PACK))
         nc.sync.dma_start(out=wb_codes[:].bitcast(I32), in_=wb_words[0].bitcast(I32))
+        nc.sync.dma_start(out=ws_rows[:], in_=ws_scales[0].bitcast(I32).rearrange("(q r) c -> r q c", r=4))
+        nc.sync.dma_start(out=wb_rows[:], in_=wb_scales[0].bitcast(I32).rearrange("(q r) c -> r q c", r=4))
         nc.sync.dma_start(page_cols[:], offs6)
 
         boards = []
@@ -81,14 +90,11 @@ def tile_list_ownsides_solo_further_scattered_kernel(
             boards.append(board)
         nc.vector.memset(ws_plane[:].bitcast(I32), 0)
         nc.vector.memset(wb_plane[:].bitcast(I32), 0)
-        load_scale_rows([nc.sync] * QUADS, ws_plane, ws_scales)
-        load_scale_rows([nc.sync] * QUADS, wb_plane, wb_scales)
 
-        for q in range(QUADS):
-            nc.vector.tensor_copy(out=w_plane_raw[32 * q : 32 * q + 4, :].bitcast(I32), in_=w_rows[:, q, :])
+        spread_scale_rows(nc, w_plane_raw, w_rows)
 
         xg_plane = keep.tile([P, J], U8, name="xg_plane", align_bytes=64)
-        xg_words = keep.tile([P, J], U32, name="xg_words", tag="w_rows_then_words", align_bytes=64)
+        xg_words = keep.tile([P, J], U32, name="xg_words", align_bytes=64)
 
         w_codes = []
         w_planes = []
@@ -136,6 +142,8 @@ def tile_list_ownsides_solo_further_scattered_kernel(
         xs_words = keep.tile([P, D], U32, name="xs_words", align_bytes=64)
         nc.vector.tensor_copy(out=xs_plane[:], in_=x_plane[:].indirect(short_tokens[:]))
         nc.vector.tensor_copy(out=xs_words[:], in_=x_words[:].bitcast(U32).indirect(short_tokens[:]))
+        spread_scale_rows(nc, ws_plane, ws_rows)
+        spread_scale_rows(nc, wb_plane, wb_rows)
         p_acc = {}
         for h in range(2):
             cols = slice(h * HALF, (h + 1) * HALF)
@@ -154,7 +162,7 @@ def tile_list_ownsides_solo_further_scattered_kernel(
         for page in pages:
             nc.vector.memset(page[:], 0.0)
 
-        hid.append(keep.tile([P, PACK, HALF], BF16, name="hid1", tag="a_rows%d_0" % (PACK - 1), align_bytes=64))
+        hid.append(keep.tile([P, PACK, HALF], BF16, name="hid1", tag="a_rows3_0", align_bytes=64))
         for t in range(PACK):
             nc.scalar.activation(
                 out=hid[1][:, t, :], in_=boards[t][:].indirect(late_places[:]), func=COPY, scale=sb_cols[:, t : t + 1]
@@ -163,18 +171,17 @@ def tile_list_ownsides_solo_further_scattered_kernel(
         def second_stage(h):
             codes = keep.tile([P, HALF], U32, name="hid_codes%d" % h, align_bytes=64)
             plane = keep.tile([P, HALF], U8, name="hid_plane%d" % h, align_bytes=64)
-            parts = []
-            for s in range(2):
-                grouped = keep.tile([P, HALF // 2, PACK], BF16, name="grouped%d%d" % (h, s), tag="grouped%d" % s, align_bytes=64)
-                cols = slice(s * (HALF // 2), (s + 1) * (HALF // 2))
+            grouped = keep.tile([P, HALF, PACK], BF16, name="grouped%d" % h, tag="grouped", align_bytes=64)
+            parts = [slice(0, HALF // 2), slice(HALF // 2, HALF)]
+            for cols in parts:
                 nc.vector.tensor_copy(
-                    out=grouped[:].rearrange("p (c i) t -> p c t i", i=4),
+                    out=grouped[:, cols, :].rearrange("p (c i) t -> p c t i", i=4),
                     in_=hid[h][:, :, cols].rearrange("p t (c i) -> p c t i", i=4),
                 )
-                parts.append((grouped, cols))
-            for grouped, cols in parts:
+            for cols in parts:
                 nc.vector.quantize_mx(
-                    out=codes[:, cols].bitcast(E4M3), scales=plane[:, cols], in_=grouped[:].rearrange("p d t -> p (d t)")
+                    out=codes[:, cols].bitcast(E4M3), scales=plane[:, cols],
+                    in_=grouped[:, cols, :].rearrange("p d t -> p (d t)"),
                 )
             for i in range(2):
                 nc.tensor.matmul_mx(

from contextlib import ExitStack

import concourse.mybir as mybir

K, T, J, R, C, O, U, D, N, E = 512, 1024, 256, 512, 512, 128, 128, 256, 256, 1024
FLOPS = 2 * K * R * J + 2 * R * N * D + 2 * K * N * D

F32 = mybir.dt.float32
BF16 = mybir.dt.bfloat16
I32 = mybir.dt.int32
U32 = mybir.dt.uint32
U16 = mybir.dt.uint16
U8 = mybir.dt.uint8
E4M3 = mybir.dt.float8_e4m3fn_x4
E5M2 = mybir.dt.float8_e5m2_x4
E2M1 = mybir.dt.float4_e2m1fn_x4
COPY = mybir.ActivationFunctionType.Copy

P = 128
PACK = 4
QUADS = 4
HALF = 128


def load_scale_rows(queues, plane, scales):
    for q in range(QUADS):
        queues[q].dma_start(out=plane[32 * q : 32 * q + 4, :].bitcast(I32), in_=scales[0, 4 * q : 4 * q + 4, :].bitcast(I32))


def spread_scale_rows(nc, plane, rows):
    for q in range(QUADS):
        nc.vector.tensor_copy(out=plane[32 * q : 32 * q + 4, :].bitcast(I32), in_=rows[:, q, :])


def tile_list_ownsides_solo_further_scattered_kernel(
    tc, xt_words, xt_scales, w_words, w_scales, sa, sb, wb_words, wb_scales, ws_words, ws_scales,
    offs, offs2, offs3, offs4, offs5, offs6, out,
):
    nc = tc.nc
    with ExitStack() as ctx:
        keep = ctx.enter_context(tc.tile_pool(name="keep", bufs=1))
        psum = ctx.enter_context(tc.psum_pool(name="psum", bufs=1))

        slots = keep.tile([P, J // 16], U16, name="slots")
        board_cols = keep.tile([P, J // 16], U16, name="board_cols")
        places = keep.tile([P, O // 16], U16, name="places")
        late_places = keep.tile([P, U // 16], U16, name="late_places")
        short_tokens = keep.tile([P, D // 16], U16, name="short_tokens")
        page_cols = keep.tile([P, D // 16], U16, name="page_cols")

        x_words = keep.tile([P, T], I32, name="x_words", tag="x_words_then_page", align_bytes=64)
        x_plane = keep.tile([P, T], U8, name="x_plane", tag="x_plane_then_page", align_bytes=64)
        w_raw = keep.tile([P, 2 * R], U8, name="w_raw", align_bytes=64)
        w_rows = keep.tile([4, QUADS, R // 4], I32, name="w_rows", align_bytes=64)
        w_plane_raw = keep.tile([P, R], U8, name="w_plane_raw", align_bytes=64)
        wb_codes = keep.tile([P, 2 * N], U8, name="wb_codes", align_bytes=64)
        wb_plane = keep.tile([P, N], U8, name="wb_plane", align_bytes=64)
        ws_codes = keep.tile([P, 2 * N], U8, name="ws_codes", align_bytes=64)
        ws_plane = keep.tile([P, N], U8, name="ws_plane", align_bytes=64)
        ws_rows = keep.tile([4, QUADS, N // 4], I32, name="ws_rows", align_bytes=64)
        wb_rows = keep.tile([4, QUADS, N // 4], I32, name="wb_rows", tag="grouped", align_bytes=64)
        sa_cols = keep.tile([P, PACK], F32, name="sa_cols")
        sb_cols = keep.tile([P, PACK], F32, name="sb_cols")

        nc.vector.memset(x_plane[:].bitcast(I32), 0)
        nc.vector.memset(w_plane_raw[:].bitcast(I32), 0)

        x_words_hbm = xt_words[0].rearrange("p n t -> p (n t)").bitcast(I32)
        nc.sync.dma_start(out=w_rows[:], in_=w_scales[0].bitcast(I32).rearrange("(q r) c -> r q c", r=4))
        nc.scalar.dma_start(out=x_words[:], in_=x_words_hbm)
        load_scale_rows([nc.sync] * QUADS, x_plane, xt_scales)
        nc.sync.dma_start(slots[:], offs)
        nc.sync.dma_start(out=w_raw[:].bitcast(I32), in_=w_words[0].bitcast(I32))
        nc.sync.dma_start(board_cols[:], offs2)
        nc.sync.dma_start(places[:], offs3)
        nc.sync.dma_start(out=sa_cols[:], in_=sa.rearrange("(p t) o -> p (t o)", t=PACK))
        nc.sync.dma_start(short_tokens[:], offs5)
        nc.sync.dma_start(out=ws_codes[:].bitcast(I32), in_=ws_words[0].bitcast(I32))
        nc.sync.dma_start(late_places[:], offs4)
        nc.sync.dma_start(out=sb_cols[:], in_=sb.rearrange("(p t) o -> p (t o)", t=PACK))
        nc.sync.dma_start(out=wb_codes[:].bitcast(I32), in_=wb_words[0].bitcast(I32))
        nc.sync.dma_start(out=ws_rows[:], in_=ws_scales[0].bitcast(I32).rearrange("(q r) c -> r q c", r=4))
        nc.sync.dma_start(out=wb_rows[:], in_=wb_scales[0].bitcast(I32).rearrange("(q r) c -> r q c", r=4))
        nc.sync.dma_start(page_cols[:], offs6)

        boards = []
        for t in range(PACK):
            board = keep.tile([P, C], F32, name="board%d" % t)
            nc.vector.memset(board[:], 0.0)
            boards.append(board)
        nc.vector.memset(ws_plane[:].bitcast(I32), 0)
        nc.vector.memset(wb_plane[:].bitcast(I32), 0)

        spread_scale_rows(nc, w_plane_raw, w_rows)

        xg_plane = keep.tile([P, J], U8, name="xg_plane", align_bytes=64)
        xg_words = keep.tile([P, J], U32, name="xg_words", align_bytes=64)

        w_codes = []
        w_planes = []

        def deal(t):
            codes = keep.tile([P, 2 * P], U8, name="w_codes%d" % t, align_bytes=64)
            plane = keep.tile([P, P], U8, name="w_plane%d" % t, align_bytes=64)
            nc.vector.tensor_copy(out=plane[:], in_=w_plane_raw[:, t::PACK])
            nc.scalar.copy(out=codes[:].bitcast(U16), in_=w_raw[:].bitcast(U16)[:, t::PACK])
            w_codes.append(codes)
            w_planes.append(plane)

        def first_product(t, first, count, tag, copy_out):
            cols = slice(first, first + count)
            acc = psum.tile([P, count], F32, name="a_acc%d_%d" % (t, first), tag=tag)
            nc.tensor.matmul_mx(
                out=acc[:], lhsT=w_codes[t][:].bitcast(E2M1), lhsT_scale=w_planes[t][:],
                rhs=xg_words[:, cols].bitcast(E5M2), rhs_scale=xg_plane[:, cols], start=True, stop=True,
            )
            a_rows = keep.tile([P, count], F32, name="a_rows%d_%d" % (t, first), tag="a_rows%d_%d" % (t, first), align_bytes=64)
            copy_out(out=a_rows[:], in_=acc[:])
            entries = board_cols[:, first // 16 : (first + count) // 16]
            nc.scalar.activation(out=boards[t][:].indirect(entries), in_=a_rows[:], func=COPY)

        deal(0)
        for first in (0, HALF):
            entries = slots[:, first // 16 : (first + HALF) // 16]
            nc.vector.tensor_copy(out=xg_plane[:, first : first + HALF], in_=x_plane[:].indirect(entries))
            nc.vector.tensor_copy(out=xg_words[:, first : first + HALF], in_=x_words[:].bitcast(U32).indirect(entries))
            first_product(0, first, HALF, "bank_a0_%d" % first, nc.scalar.copy if first == 0 else nc.vector.tensor_copy)
            if first == 0:
                deal(1)
            first_product(1, first, HALF, "bank_a1_%d" % first, nc.vector.tensor_copy)
        for t in range(2, PACK):
            deal(t)
            first_product(t, 0, J, "bank_a%d" % t, nc.vector.tensor_copy)

        hid = [keep.tile([P, PACK, HALF], BF16, name="hid0", tag="a_rows2_0", align_bytes=64)]
        for t in range(PACK):
            nc.scalar.activation(
                out=hid[0][:, t, :], in_=boards[t][:].indirect(places[:]), func=COPY, scale=sa_cols[:, t : t + 1]
            )

        xs_plane = keep.tile([P, D], U8, name="xs_plane", align_bytes=64)
        xs_words = keep.tile([P, D], U32, name="xs_words", align_bytes=64)
        nc.vector.tensor_copy(out=xs_plane[:], in_=x_plane[:].indirect(short_tokens[:]))
        nc.vector.tensor_copy(out=xs_words[:], in_=x_words[:].bitcast(U32).indirect(short_tokens[:]))
        spread_scale_rows(nc, ws_plane, ws_rows)
        spread_scale_rows(nc, wb_plane, wb_rows)
        p_acc = {}
        for h in range(2):
            cols = slice(h * HALF, (h + 1) * HALF)
            for i in range(2):
                acc = psum.tile([P, HALF], F32, name="p_acc%d%d" % (h, i), tag="bank_a%d_0" % i if h == 1 else "bank_p%d" % i)
                nc.tensor.matmul_mx(
                    out=acc[:], lhsT=ws_codes[:, 2 * P * i : 2 * P * (i + 1)].bitcast(E2M1),
                    lhsT_scale=ws_plane[:, P * i : P * (i + 1)],
                    rhs=xs_words[:, cols].bitcast(E5M2), rhs_scale=xs_plane[:, cols], start=True, stop=False,
                )
                p_acc[(h, i)] = acc

        page0 = keep.tile([P, E], F32, name="page0", tag="x_words_then_page", align_bytes=64)
        page1 = keep.tile([P, E], F32, name="page1", tag="x_plane_then_page", align_bytes=64)
        pages = [page0, page1]
        for page in pages:
            nc.vector.memset(page[:], 0.0)

        hid.append(keep.tile([P, PACK, HALF], BF16, name="hid1", tag="a_rows3_0", align_bytes=64))
        for t in range(PACK):
            nc.scalar.activation(
                out=hid[1][:, t, :], in_=boards[t][:].indirect(late_places[:]), func=COPY, scale=sb_cols[:, t : t + 1]
            )

        def second_stage(h):
            codes = keep.tile([P, HALF], U32, name="hid_codes%d" % h, align_bytes=64)
            plane = keep.tile([P, HALF], U8, name="hid_plane%d" % h, align_bytes=64)
            grouped = keep.tile([P, HALF, PACK], BF16, name="grouped%d" % h, tag="grouped", align_bytes=64)
            parts = [slice(0, HALF // 2), slice(HALF // 2, HALF)]
            for cols in parts:
                nc.vector.tensor_copy(
                    out=grouped[:, cols, :].rearrange("p (c i) t -> p c t i", i=4),
                    in_=hid[h][:, :, cols].rearrange("p t (c i) -> p c t i", i=4),
                )
            for cols in parts:
                nc.vector.quantize_mx(
                    out=codes[:, cols].bitcast(E4M3), scales=plane[:, cols],
                    in_=grouped[:, cols, :].rearrange("p d t -> p (d t)"),
                )
            for i in range(2):
                nc.tensor.matmul_mx(
                    out=p_acc[(h, i)][:], lhsT=wb_codes[:, 2 * P * i : 2 * P * (i + 1)].bitcast(E2M1),
                    lhsT_scale=wb_plane[:, P * i : P * (i + 1)],
                    rhs=codes[:].bitcast(E4M3), rhs_scale=plane[:], start=False, stop=True,
                )

        def put(h, rows0, rows1):
            entries = page_cols[:, h * (HALF // 16) : (h + 1) * (HALF // 16)]
            nc.scalar.copy(out=rows0, in_=p_acc[(h, 0)][:])
            nc.scalar.copy(out=rows1, in_=p_acc[(h, 1)][:])
            nc.scalar.activation(out=page0[:].indirect(entries), in_=rows0, func=COPY)
            nc.vector.tensor_copy(out=page1[:].indirect(entries), in_=rows1)

        second_stage(0)
        second_stage(1)
        early0 = keep.tile([P, HALF], F32, name="early0", tag="p_rows")
        early1 = keep.tile([P, HALF], F32, name="early1")
        put(0, early0[:], early1[:])
        late = keep.tile([P, 2, HALF], F32, name="late", tag="p_rows")
        put(1, late[:, 0, :], late[:, 1, :])
        nc.sync.dma_start(out=out[P : 2 * P, :], in_=page1[:])
        nc.scalar.dma_start(out=out[0:P, :], in_=page0[:])
